import numpy as np, ml_dtypes
CORES = [21,29,37,45,53,61,69,77,85]
N = 9
GR, GC, HH, WW = 3, 3, 8, 32
def setup_inputs(rng):
    return {"x": rng.standard_normal((N, 128, HH * WW), dtype=np.float32).astype(ml_dtypes.bfloat16), "w": rng.standard_normal((N, 128, 9 * 128), dtype=np.float32).astype(ml_dtypes.bfloat16)}
def reference(x, w):
    X = x.astype(np.float64).reshape(GR, GC, 128, HH, WW); W = w.astype(np.float64)
    g = np.concatenate([np.concatenate(list(X[i]), axis=2) for i in range(GR)], axis=1)
    y = np.zeros((N, 128, HH * WW))
    for r in range(N):
        i0, j0 = HH * (r // GC), WW * (r % GC)
        for a in range(3):
            for b in range(3):
                sh = np.roll(g, (-2 * (a - 1), -2 * (b - 1)), axis=(1, 2))[:, i0:i0 + HH, j0:j0 + WW]
                y[r] += W[r][:, 128 * (3 * a + b):128 * (3 * a + b) + 128].T @ sh.reshape(128, HH * WW)
    return {"y": y.astype(ml_dtypes.bfloat16 if x.dtype != np.float64 else np.float64)}

@@ -1,0 +1,198 @@
+from concourse.bass import DstId, RemoteDMATransfer
+
+NSIM = 96
+GR, GC = 3, 3
+SCRATCH = {
+    "xs": ("sbuf", [128, 8, 16, 2], "bfloat16"),
+    "ws": ("sbuf", [128, 1152], "bfloat16"),
+    "pk": ("sbuf", [128, 16, 2, 2], "bfloat16"),
+    "ht": ("sbuf", [128, 2, 16, 2], "bfloat16"),
+    "hb": ("sbuf", [128, 2, 16, 2], "bfloat16"),
+    "hl": ("sbuf", [128, 24, 2, 2], "bfloat16"),
+    "hr": ("sbuf", [128, 24, 2, 2], "bfloat16"),
+    "acc": ("psum", [128, 8, 16, 2], "float32"),
+    "ys": ("sbuf", [128, 8, 16, 2], "bfloat16"),
+}
+SEMAPHORES = ["ldx", "ldw", "pkd", "sent", "hand", "arrd", "arrr", "mm", "cpd", "std"]
+
+
+def _bits(m):
+    return [e for e in range(m.bit_length()) if (m >> e) & 1]
+
+
+def _mask(es):
+    m = 0
+    for e in es:
+        m |= 1 << e
+    return m
+
+
+def _engines(topo, src, dsts):
+    m = topo.mask(src, dsts[0])
+    for d in dsts[1:]:
+        m &= topo.mask(src, d)
+    return _bits(m)
+
+
+def _plan(T, topo):
+    cores = list(T.cores)
+    calls, arrive, via = {}, {}, {}
+
+    def add(core, call):
+        calls.setdefault(core, []).append(call)
+        for (_p, _w, dsts, es, sem) in call:
+            for (d, _b, _s) in dsts:
+                arrive[(d, sem)] = arrive.get((d, sem), 0) + len(es)
+
+    for s, c in enumerate(cores):
+        gr, gc = divmod(s, GC)
+        near = {"pk": [], "top": [], "bot": []}
+        far = {"pk": [], "top": [], "bot": []}
+        for dr in (-1, 0, 1):
+            for dc in (-1, 0, 1):
+                if dr == 0 and dc == 0:
+                    continue
+                d = ((gr + dr) % GR) * GC + (gc + dc) % GC
+                if dc == 0:
+                    piece, m = ("top", (cores[d], "hb", None)) if dr < 0 else ("bot", (cores[d], "ht", None))
+                else:
+                    piece, m = "pk", (cores[d], "hl" if dc > 0 else "hr", 1 - dr)
+                ok = topo.may_write(c, cores[d])
+                (near if ok else far)[piece].append(m)
+                via[(s, d)] = "arrd" if ok else "arrr"
+        fardst = [m[0] for p in far for m in far[p]]
+        cand = [h for h in range(NSIM) if topo.chip(h) == topo.chip(c) and T.rank_of(h) is None
+                and all(topo.may_write(h, d) for d in fardst)]
+        cand.sort(key=lambda h: (topo.die(h) != topo.die(c), h))
+        half = (len(far["pk"]) + 1) // 2
+        jobs = [("pk", part) for part in (far["pk"][:half], far["pk"][half:]) if part]
+        jobs += [(p, far[p]) for p in ("top", "bot") if far[p]]
+        jobs = [(cand[i], p, ms) for i, (p, ms) in enumerate(jobs)]
+        on = _engines(topo, c, [h for (h, _p, _m) in jobs])
+        lo, hi = on[:len(on) // 2], on[len(on) // 2:]
+        first = []
+        hp = [h for (h, p, _m) in jobs if p == "pk"]
+        if hp:
+            first.append(("pk", True, [(h, "pk", None) for h in hp], lo, "hand"))
+        ha = [(h, p) for (h, p, _m) in jobs if p != "pk"]
+        for i, (h, p) in enumerate(ha):
+            n = len(hi) // len(ha)
+            first.append((p, True, [(h, p, None)], hi[i * n:(i + 1) * n], "hand"))
+        add(c, first)
+        for (h, p, ms) in jobs:
+            add(h, [(p, False, ms, _engines(topo, h, [m[0] for m in ms]), "arrr")])
+        if near["pk"]:
+            add(c, [("pk", False, near["pk"], _engines(topo, c, [m[0] for m in near["pk"]]), "arrd")])
+        na = [(p, near[p]) for p in ("top", "bot") if near[p]]
+        if na:
+            off = _engines(topo, c, [m[0] for (_p, ms) in na for m in ms])
+            n = len(off) // len(na)
+            add(c, [(p, False, ms, off[i * n:(i + 1) * n], "arrd") for i, (p, ms) in enumerate(na)])
+    return calls, arrive, via
+
+
+def _piece(T, piece, wide):
+    if piece == "top":
+        return T.xs[:, 0:2, :, :]
+    if piece == "bot":
+        return T.xs[:, 6:8, :, :]
+    return T.pk[:, :, :, :] if wide else T.pk[:, 0:8, :, :]
+
+
+def _land(T, buf, slot, wide):
+    if buf in ("top", "bot", "pk"):
+        return _piece(T, buf, wide)
+    if slot is None:
+        return T[buf][:, :, :, :]
+    return T[buf][:, 8 * slot:8 * slot + 8, :, :]
+
+
+def _issue(g, T, topo, call):
+    trs = []
+    for (p, wide, dsts, es, sem) in call:
+        ids = []
+        for (d, _b, _s) in dsts:
+            rid, pid, _se = topo.addr(d)
+            ids.append(DstId(rid=rid, pnc=pid))
+        trs.append(RemoteDMATransfer(dst_ids=ids, dma_engine_mask=_mask(es), remote_sem=T.sem[sem],
+                                     srcs=[_piece(T, p, wide)], dsts=[_land(T, b, s, wide) for (_d, b, s) in dsts],
+                                     alu_op=0))
+    g.remote_dma_fused(trs, local_sem=T.sem.sent)
+    return sum(len(es) for (_p, _w, _d, es, _s) in call)
+
+
+def rank_program(g, core, T, topo):
+    calls, arrive, via = _plan(T, topo)
+    rank = T.rank_of(core)
+    S = T.sem
+    if rank is None:
+        if core not in calls:
+            return
+        g.wait_ge(S.hand, arrive[(core, "hand")])
+        n = 0
+        for call in calls[core]:
+            n += _issue(g, T, topo, call)
+        g.wait_ge(S.sent, n)
+        return
+
+    g.sync.dma_start(T.xs[:, :, :, :], T.x[:, :]).then_inc(S.ldx, 16)
+    g.sync.dma_start(T.ws[:, :], T.w[:, :]).then_inc(S.ldw, 16)
+
+    g.vector.memset(T.pk[:, 8:16, :, :], 0.0).then_inc(S.pkd, 1)
+    g.vector.wait_ge(S.ldx, 16)
+    g.vector.tensor_copy(T.pk[:, 0:8, :, :], T.xs[:, :, 0:16:15, :]).then_inc(S.pkd, 1)
+
+    g.wait_ge(S.ldx, 16)
+    g.wait_ge(S.pkd, 2)
+    nsent = 0
+    for call in calls[core]:
+        nsent += _issue(g, T, topo, call)
+
+    gr, gc = divmod(rank, GC)
+
+    def nb(dr, dc):
+        return ((gr + dr) % GR) * GC + (gc + dc) % GC
+
+    own, halo = [], []
+    for a in (1, 0, 2):
+        for b in (1, 0, 2):
+            W = T.ws[:, 128 * (3 * a + b):128 * (3 * a + b) + 128]
+            di, dq = 2 * (a - 1), b - 1
+            o0, o1 = max(0, -di), min(8, 8 - di)
+            p0, p1 = max(0, -dq), min(16, 16 - dq)
+            own.append((T.acc[:, o0:o1, p0:p1, :], W, T.xs[:, o0 + di:o1 + di, p0 + dq:p1 + dq, :]))
+            if a == 0:
+                halo.append(([nb(-1, 0)], T.acc[:, 0:2, p0:p1, :], W, T.ht[:, :, p0 + dq:p1 + dq, :]))
+            if a == 2:
+                halo.append(([nb(1, 0)], T.acc[:, 6:8, p0:p1, :], W, T.hb[:, :, p0 + dq:p1 + dq, :]))
+            if b != 1:
+                src = [nb(0, dq)] + ([nb(a - 1, dq)] if a != 1 else [])
+                if b == 0:
+                    halo.append((src, T.acc[:, :, 0:1, :], W, T.hl[:, 6 + 2 * a:14 + 2 * a, 1:2, :]))
+                else:
+                    halo.append((src, T.acc[:, :, 15:16, :], W, T.hr[:, 6 + 2 * a:14 + 2 * a, 0:1, :]))
+    early = [h for h in halo if all(via[(s, rank)] == "arrd" for s in h[0])]
+    late = [h for h in halo if not all(via[(s, rank)] == "arrd" for s in h[0])]
+    total = len(own) + len(halo)
+    te = g.tensor
+    te.wait_ge(S.ldx, 16)
+    te.wait_ge(S.ldw, 16)
+    k = 0
+    for (out, W, rhs) in own:
+        te.matmul(out, W, rhs, start=(k == 0), stop=False).then_inc(S.mm, 1)
+        k += 1
+    te.wait_ge(S.arrd, arrive[(core, "arrd")])
+    for (_s, out, W, rhs) in early:
+        k += 1
+        te.matmul(out, W, rhs, start=False, stop=(k == total)).then_inc(S.mm, 1)
+    te.wait_ge(S.arrr, arrive[(core, "arrr")])
+    for (_s, out, W, rhs) in late:
+        k += 1
+        te.matmul(out, W, rhs, start=False, stop=(k == total)).then_inc(S.mm, 1)
+
+    g.vector.wait_ge(S.mm, total)
+    g.vector.tensor_copy(T.ys[:, :, :, :], T.acc[:, :, :, :]).then_inc(S.cpd, 1)
+    g.sync.wait_ge(S.cpd, 1)
+    g.sync.dma_start(T.y[:, :], T.ys[:, :, :, :]).then_inc(S.std, 16)
+    g.sync.wait_ge(S.std, 16)
+    g.wait_ge(S.sent, nsent)

@@ -1,19 +1,25 @@
 from concourse.bass import DstId, RemoteDMATransfer
+from concourse.mybir import AluOpType
 
 NSIM = 96
 GR, GC = 3, 3
 SCRATCH = {
     "xs": ("sbuf", [128, 8, 16, 2], "bfloat16"),
     "ws": ("sbuf", [128, 1152], "bfloat16"),
-    "pk": ("sbuf", [128, 16, 2, 2], "bfloat16"),
+    "pk": ("sbuf", [128, 8, 2, 2], "bfloat16"),
     "ht": ("sbuf", [128, 2, 16, 2], "bfloat16"),
     "hb": ("sbuf", [128, 2, 16, 2], "bfloat16"),
     "hl": ("sbuf", [128, 24, 2, 2], "bfloat16"),
     "hr": ("sbuf", [128, 24, 2, 2], "bfloat16"),
-    "acc": ("psum", [128, 8, 16, 2], "float32"),
+    "acc": ("psum", [128, 16, 16, 2], "float32"),
+    "acce": ("psum", [128, 128, 2, 2], "float32"),
+    "te": ("sbuf", [128, 8, 2, 2], "float32"),
     "ys": ("sbuf", [128, 8, 16, 2], "bfloat16"),
 }
-SEMAPHORES = ["ldx", "ldw", "pkd", "sent", "hand", "arrd", "arrr", "mm", "cpd", "std"]
+WPIECES = [(4, 6), (2, 4), (0, 2), (6, 8), (8, 9)]
+KINDS = ["dtb", "ftb", "dpk", "fpk"]
+SEMAPHORES = (["ldx", "pkd", "sent", "hand", "zed", "mm", "me", "cpe", "cpd", "std"] + KINDS
+              + ["lw%d" % i for i in range(len(WPIECES))])
 
 
 def _bits(m):
@@ -40,7 +46,7 @@ def _plan(T, topo):
 
     def add(core, call):
         calls.setdefault(core, []).append(call)
-        for (_p, _w, dsts, es, sem) in call:
+        for (_p, dsts, es, sem) in call:
             for (d, _b, _s) in dsts:
                 arrive[(d, sem)] = arrive.get((d, sem), 0) + len(es)
 
@@ -59,7 +65,7 @@ def _plan(T, topo):
                     piece, m = "pk", (cores[d], "hl" if dc > 0 else "hr", 1 - dr)
                 ok = topo.may_write(c, cores[d])
                 (near if ok else far)[piece].append(m)
-                via[(s, d)] = "arrd" if ok else "arrr"
+                via[(s, d)] = ("d" if ok else "f") + ("pk" if piece == "pk" else "tb")
         fardst = [m[0] for p in far for m in far[p]]
         cand = [h for h in range(NSIM) if topo.chip(h) == topo.chip(c) and T.rank_of(h) is None
                 and all(topo.may_write(h, d) for d in fardst)]
@@ -70,38 +76,33 @@ def _plan(T, topo):
         jobs = [(cand[i], p, ms) for i, (p, ms) in enumerate(jobs)]
         on = _engines(topo, c, [h for (h, _p, _m) in jobs])
         lo, hi = on[:len(on) // 2], on[len(on) // 2:]
-        first = []
         hp = [h for (h, p, _m) in jobs if p == "pk"]
-        if hp:
-            first.append(("pk", True, [(h, "pk", None) for h in hp], lo, "hand"))
         ha = [(h, p) for (h, p, _m) in jobs if p != "pk"]
-        for i, (h, p) in enumerate(ha):
-            n = len(hi) // len(ha)
-            first.append((p, True, [(h, p, None)], hi[i * n:(i + 1) * n], "hand"))
-        add(c, first)
+        n = len(hi) // len(ha)
+        add(c, [(p, [(h, p, None)], hi[i * n:(i + 1) * n], "hand") for i, (h, p) in enumerate(ha)])
+        add(c, [("pk", [(h, "pk", None) for h in hp], lo, "hand")])
         for (h, p, ms) in jobs:
-            add(h, [(p, False, ms, _engines(topo, h, [m[0] for m in ms]), "arrr")])
-        if near["pk"]:
-            add(c, [("pk", False, near["pk"], _engines(topo, c, [m[0] for m in near["pk"]]), "arrd")])
+            add(h, [(p, ms, _engines(topo, h, [m[0] for m in ms]), "fpk" if p == "pk" else "ftb")])
         na = [(p, near[p]) for p in ("top", "bot") if near[p]]
         if na:
             off = _engines(topo, c, [m[0] for (_p, ms) in na for m in ms])
             n = len(off) // len(na)
-            add(c, [(p, False, ms, off[i * n:(i + 1) * n], "arrd") for i, (p, ms) in enumerate(na)])
+            add(c, [(p, ms, off[i * n:(i + 1) * n], "dtb") for i, (p, ms) in enumerate(na)])
+        add(c, [("pk", near["pk"], _engines(topo, c, [m[0] for m in near["pk"]]), "dpk")])
     return calls, arrive, via
 
 
-def _piece(T, piece, wide):
+def _piece(T, piece):
     if piece == "top":
         return T.xs[:, 0:2, :, :]
     if piece == "bot":
         return T.xs[:, 6:8, :, :]
-    return T.pk[:, :, :, :] if wide else T.pk[:, 0:8, :, :]
+    return T.pk[:, :, :, :]
 
 
-def _land(T, buf, slot, wide):
+def _land(T, buf, slot):
     if buf in ("top", "bot", "pk"):
-        return _piece(T, buf, wide)
+        return _piece(T, buf)
     if slot is None:
         return T[buf][:, :, :, :]
     return T[buf][:, 8 * slot:8 * slot + 8, :, :]
@@ -109,16 +110,16 @@ def _land(T, buf, slot, wide):
 
 def _issue(g, T, topo, call):
     trs = []
-    for (p, wide, dsts, es, sem) in call:
+    for (p, dsts, es, sem) in call:
         ids = []
         for (d, _b, _s) in dsts:
             rid, pid, _se = topo.addr(d)
             ids.append(DstId(rid=rid, pnc=pid))
         trs.append(RemoteDMATransfer(dst_ids=ids, dma_engine_mask=_mask(es), remote_sem=T.sem[sem],
-                                     srcs=[_piece(T, p, wide)], dsts=[_land(T, b, s, wide) for (_d, b, s) in dsts],
+                                     srcs=[_piece(T, p)], dsts=[_land(T, b, s) for (_d, b, s) in dsts],
                                      alu_op=0))
     g.remote_dma_fused(trs, local_sem=T.sem.sent)
-    return sum(len(es) for (_p, _w, _d, es, _s) in call)
+    return sum(len(es) for (_p, _d, es, _s) in call)
 
 
 def rank_program(g, core, T, topo):
@@ -136,16 +137,20 @@ def rank_program(g, core, T, topo):
         return
 
     g.sync.dma_start(T.xs[:, :, :, :], T.x[:, :]).then_inc(S.ldx, 16)
-    g.sync.dma_start(T.ws[:, :], T.w[:, :]).then_inc(S.ldw, 16)
+    for i, (t0, t1) in enumerate(WPIECES):
+        g.sync.dma_start(T.ws[:, 128 * t0:128 * t1], T.w[:, 128 * t0:128 * t1]).then_inc(S["lw%d" % i], 16)
 
-    g.vector.memset(T.pk[:, 8:16, :, :], 0.0).then_inc(S.pkd, 1)
+    g.vector.memset(T.acce[:, 0:8, :, :], 0.0).then_inc(S.zed, 1)
     g.vector.wait_ge(S.ldx, 16)
-    g.vector.tensor_copy(T.pk[:, 0:8, :, :], T.xs[:, :, 0:16:15, :]).then_inc(S.pkd, 1)
+    g.vector.tensor_copy(T.pk[:, :, :, :], T.xs[:, :, 0:16:15, :]).then_inc(S.pkd, 1)
 
     g.wait_ge(S.ldx, 16)
-    g.wait_ge(S.pkd, 2)
     nsent = 0
+    packed = False
     for call in calls[core]:
+        if not packed and any(p == "pk" for (p, _d, _e, _s) in call):
+            g.wait_ge(S.pkd, 1)
+            packed = True
         nsent += _issue(g, T, topo, call)
 
     gr, gc = divmod(rank, GC)
@@ -153,46 +158,62 @@ def rank_program(g, core, T, topo):
     def nb(dr, dc):
         return ((gr + dr) % GR) * GC + (gc + dc) % GC
 
-    own, halo = [], []
-    for a in (1, 0, 2):
-        for b in (1, 0, 2):
-            W = T.ws[:, 128 * (3 * a + b):128 * (3 * a + b) + 128]
+    own, rows, strips = [], [], []
+    for (t0, t1) in WPIECES:
+        part = []
+        for t in range(t0, t1):
+            a, b = divmod(t, 3)
+            W = T.ws[:, 128 * t:128 * t + 128]
             di, dq = 2 * (a - 1), b - 1
             o0, o1 = max(0, -di), min(8, 8 - di)
             p0, p1 = max(0, -dq), min(16, 16 - dq)
-            own.append((T.acc[:, o0:o1, p0:p1, :], W, T.xs[:, o0 + di:o1 + di, p0 + dq:p1 + dq, :]))
+            part.append((T.acc[:, o0:o1, p0:p1, :], W, T.xs[:, o0 + di:o1 + di, p0 + dq:p1 + dq, :]))
             if a == 0:
-                halo.append(([nb(-1, 0)], T.acc[:, 0:2, p0:p1, :], W, T.ht[:, :, p0 + dq:p1 + dq, :]))
+                rows.append((via[(nb(-1, 0), rank)], T.acc[:, 0:2, p0:p1, :], W, T.ht[:, :, p0 + dq:p1 + dq, :]))
             if a == 2:
-                halo.append(([nb(1, 0)], T.acc[:, 6:8, p0:p1, :], W, T.hb[:, :, p0 + dq:p1 + dq, :]))
+                rows.append((via[(nb(1, 0), rank)], T.acc[:, 6:8, p0:p1, :], W, T.hb[:, :, p0 + dq:p1 + dq, :]))
             if b != 1:
                 src = [nb(0, dq)] + ([nb(a - 1, dq)] if a != 1 else [])
+                kind = KINDS[max(KINDS.index(via[(s, rank)]) for s in src)]
                 if b == 0:
-                    halo.append((src, T.acc[:, :, 0:1, :], W, T.hl[:, 6 + 2 * a:14 + 2 * a, 1:2, :]))
+                    strips.append((kind, T.acce[:, 0:8, 0:1, :], W, T.hl[:, 6 + 2 * a:14 + 2 * a, 1:2, :]))
                 else:
-                    halo.append((src, T.acc[:, :, 15:16, :], W, T.hr[:, 6 + 2 * a:14 + 2 * a, 0:1, :]))
-    early = [h for h in halo if all(via[(s, rank)] == "arrd" for s in h[0])]
-    late = [h for h in halo if not all(via[(s, rank)] == "arrd" for s in h[0])]
-    total = len(own) + len(halo)
+                    strips.append((kind, T.acce[:, 0:8, 1:2, :], W, T.hr[:, 6 + 2 * a:14 + 2 * a, 0:1, :]))
+        own.append(part)
+    nmain = sum(len(p) for p in own) + len(rows)
     te = g.tensor
     te.wait_ge(S.ldx, 16)
-    te.wait_ge(S.ldw, 16)
     k = 0
-    for (out, W, rhs) in own:
-        te.matmul(out, W, rhs, start=(k == 0), stop=False).then_inc(S.mm, 1)
-        k += 1
-    te.wait_ge(S.arrd, arrive[(core, "arrd")])
-    for (_s, out, W, rhs) in early:
-        k += 1
-        te.matmul(out, W, rhs, start=False, stop=(k == total)).then_inc(S.mm, 1)
-    te.wait_ge(S.arrr, arrive[(core, "arrr")])
-    for (_s, out, W, rhs) in late:
-        k += 1
-        te.matmul(out, W, rhs, start=False, stop=(k == total)).then_inc(S.mm, 1)
+    for i, part in enumerate(own):
+        te.wait_ge(S["lw%d" % i], 16)
+        for (out, W, rhs) in part:
+            te.matmul(out, W, rhs, start=(k == 0), stop=False).then_inc(S.mm, 1)
+            k += 1
+    for kind in ("dtb", "ftb"):
+        if (core, kind) in arrive:
+            te.wait_ge(S[kind], arrive[(core, kind)])
+            for (kd, out, W, rhs) in rows:
+                if kd == kind:
+                    k += 1
+                    te.matmul(out, W, rhs, start=False, stop=(k == nmain)).then_inc(S.mm, 1)
+    te.wait_ge(S.zed, 1)
+    k = 0
+    for kind in ("dpk", "fpk"):
+        if (core, kind) in arrive:
+            te.wait_ge(S[kind], arrive[(core, kind)])
+            for (kd, out, W, rhs) in strips:
+                if kd == kind:
+                    k += 1
+                    te.matmul(out, W, rhs, start=(k == 1), stop=(k == len(strips))).then_inc(S.me, 1)
 
-    g.vector.wait_ge(S.mm, total)
-    g.vector.tensor_copy(T.ys[:, :, :, :], T.acc[:, :, :, :]).then_inc(S.cpd, 1)
-    g.sync.wait_ge(S.cpd, 1)
+    g.vector.wait_ge(S.mm, nmain)
+    g.vector.tensor_copy(T.te[:, :, :, :], T.acc[:, 0:8, 0:16:15, :]).then_inc(S.cpe, 1)
+    g.vector.tensor_copy(T.ys[:, :, 1:15, :], T.acc[:, 0:8, 1:15, :]).then_inc(S.cpd, 1)
+    g.vector.wait_ge(S.me, len(strips))
+    g.vector.wait_ge(S.cpe, 1)
+    g.vector.tensor_tensor(T.ys[:, :, 0:16:15, :], T.acce[:, 0:8, :, :], T.te[:, :, :, :],
+                           AluOpType.add).then_inc(S.cpd, 1)
+    g.sync.wait_ge(S.cpd, 2)
     g.sync.dma_start(T.y[:, :], T.ys[:, :, :, :]).then_inc(S.std, 16)
     g.sync.wait_ge(S.std, 16)
     g.wait_ge(S.sent, nsent)

from concourse.bass import DstId, RemoteDMATransfer
from concourse.mybir import AluOpType

NSIM = 96
GR, GC = 3, 3
SCRATCH = {
    "xs": ("sbuf", [128, 8, 16, 2], "bfloat16"),
    "ws": ("sbuf", [128, 1152], "bfloat16"),
    "pk": ("sbuf", [128, 8, 2, 2], "bfloat16"),
    "ht": ("sbuf", [128, 2, 16, 2], "bfloat16"),
    "hb": ("sbuf", [128, 2, 16, 2], "bfloat16"),
    "hl": ("sbuf", [128, 24, 2, 2], "bfloat16"),
    "hr": ("sbuf", [128, 24, 2, 2], "bfloat16"),
    "acc": ("psum", [128, 16, 16, 2], "float32"),
    "acce": ("psum", [128, 128, 2, 2], "float32"),
    "te": ("sbuf", [128, 8, 2, 2], "float32"),
    "ys": ("sbuf", [128, 8, 16, 2], "bfloat16"),
}
WPIECES = [(4, 6), (2, 4), (0, 2), (6, 8), (8, 9)]
KINDS = ["dtb", "ftb", "dpk", "fpk"]
SEMAPHORES = (["ldx", "pkd", "sent", "hand", "zed", "mm", "me", "cpe", "cpd", "std"] + KINDS
              + ["lw%d" % i for i in range(len(WPIECES))])


def _bits(m):
    return [e for e in range(m.bit_length()) if (m >> e) & 1]


def _mask(es):
    m = 0
    for e in es:
        m |= 1 << e
    return m


def _engines(topo, src, dsts):
    m = topo.mask(src, dsts[0])
    for d in dsts[1:]:
        m &= topo.mask(src, d)
    return _bits(m)


def _plan(T, topo):
    cores = list(T.cores)
    calls, arrive, via = {}, {}, {}

    def add(core, call):
        calls.setdefault(core, []).append(call)
        for (_p, dsts, es, sem) in call:
            for (d, _b, _s) in dsts:
                arrive[(d, sem)] = arrive.get((d, sem), 0) + len(es)

    for s, c in enumerate(cores):
        gr, gc = divmod(s, GC)
        near = {"pk": [], "top": [], "bot": []}
        far = {"pk": [], "top": [], "bot": []}
        for dr in (-1, 0, 1):
            for dc in (-1, 0, 1):
                if dr == 0 and dc == 0:
                    continue
                d = ((gr + dr) % GR) * GC + (gc + dc) % GC
                if dc == 0:
                    piece, m = ("top", (cores[d], "hb", None)) if dr < 0 else ("bot", (cores[d], "ht", None))
                else:
                    piece, m = "pk", (cores[d], "hl" if dc > 0 else "hr", 1 - dr)
                ok = topo.may_write(c, cores[d])
                (near if ok else far)[piece].append(m)
                via[(s, d)] = ("d" if ok else "f") + ("pk" if piece == "pk" else "tb")
        fardst = [m[0] for p in far for m in far[p]]
        cand = [h for h in range(NSIM) if topo.chip(h) == topo.chip(c) and T.rank_of(h) is None
                and all(topo.may_write(h, d) for d in fardst)]
        cand.sort(key=lambda h: (topo.die(h) != topo.die(c), h))
        half = (len(far["pk"]) + 1) // 2
        jobs = [("pk", part) for part in (far["pk"][:half], far["pk"][half:]) if part]
        jobs += [(p, far[p]) for p in ("top", "bot") if far[p]]
        jobs = [(cand[i], p, ms) for i, (p, ms) in enumerate(jobs)]
        on = _engines(topo, c, [h for (h, _p, _m) in jobs])
        lo, hi = on[:len(on) // 2], on[len(on) // 2:]
        hp = [h for (h, p, _m) in jobs if p == "pk"]
        ha = [(h, p) for (h, p, _m) in jobs if p != "pk"]
        n = len(hi) // len(ha)
        add(c, [(p, [(h, p, None)], hi[i * n:(i + 1) * n], "hand") for i, (h, p) in enumerate(ha)])
        add(c, [("pk", [(h, "pk", None) for h in hp], lo, "hand")])
        for (h, p, ms) in jobs:
            add(h, [(p, ms, _engines(topo, h, [m[0] for m in ms]), "fpk" if p == "pk" else "ftb")])
        na = [(p, near[p]) for p in ("top", "bot") if near[p]]
        if na:
            off = _engines(topo, c, [m[0] for (_p, ms) in na for m in ms])
            n = len(off) // len(na)
            add(c, [(p, ms, off[i * n:(i + 1) * n], "dtb") for i, (p, ms) in enumerate(na)])
        add(c, [("pk", near["pk"], _engines(topo, c, [m[0] for m in near["pk"]]), "dpk")])
    return calls, arrive, via


def _piece(T, piece):
    if piece == "top":
        return T.xs[:, 0:2, :, :]
    if piece == "bot":
        return T.xs[:, 6:8, :, :]
    return T.pk[:, :, :, :]


def _land(T, buf, slot):
    if buf in ("top", "bot", "pk"):
        return _piece(T, buf)
    if slot is None:
        return T[buf][:, :, :, :]
    return T[buf][:, 8 * slot:8 * slot + 8, :, :]


def _issue(g, T, topo, call):
    trs = []
    for (p, dsts, es, sem) in call:
        ids = []
        for (d, _b, _s) in dsts:
            rid, pid, _se = topo.addr(d)
            ids.append(DstId(rid=rid, pnc=pid))
        trs.append(RemoteDMATransfer(dst_ids=ids, dma_engine_mask=_mask(es), remote_sem=T.sem[sem],
                                     srcs=[_piece(T, p)], dsts=[_land(T, b, s) for (_d, b, s) in dsts],
                                     alu_op=0))
    g.remote_dma_fused(trs, local_sem=T.sem.sent)
    return sum(len(es) for (_p, _d, es, _s) in call)


def rank_program(g, core, T, topo):
    calls, arrive, via = _plan(T, topo)
    rank = T.rank_of(core)
    S = T.sem
    if rank is None:
        if core not in calls:
            return
        g.wait_ge(S.hand, arrive[(core, "hand")])
        n = 0
        for call in calls[core]:
            n += _issue(g, T, topo, call)
        g.wait_ge(S.sent, n)
        return

    g.sync.dma_start(T.xs[:, :, :, :], T.x[:, :]).then_inc(S.ldx, 16)
    for i, (t0, t1) in enumerate(WPIECES):
        g.sync.dma_start(T.ws[:, 128 * t0:128 * t1], T.w[:, 128 * t0:128 * t1]).then_inc(S["lw%d" % i], 16)

    g.vector.memset(T.acce[:, 0:8, :, :], 0.0).then_inc(S.zed, 1)
    g.vector.wait_ge(S.ldx, 16)
    g.vector.tensor_copy(T.pk[:, :, :, :], T.xs[:, :, 0:16:15, :]).then_inc(S.pkd, 1)

    g.wait_ge(S.ldx, 16)
    nsent = 0
    packed = False
    for call in calls[core]:
        if not packed and any(p == "pk" for (p, _d, _e, _s) in call):
            g.wait_ge(S.pkd, 1)
            packed = True
        nsent += _issue(g, T, topo, call)

    gr, gc = divmod(rank, GC)

    def nb(dr, dc):
        return ((gr + dr) % GR) * GC + (gc + dc) % GC

    own, rows, strips = [], [], []
    for (t0, t1) in WPIECES:
        part = []
        for t in range(t0, t1):
            a, b = divmod(t, 3)
            W = T.ws[:, 128 * t:128 * t + 128]
            di, dq = 2 * (a - 1), b - 1
            o0, o1 = max(0, -di), min(8, 8 - di)
            p0, p1 = max(0, -dq), min(16, 16 - dq)
            part.append((T.acc[:, o0:o1, p0:p1, :], W, T.xs[:, o0 + di:o1 + di, p0 + dq:p1 + dq, :]))
            if a == 0:
                rows.append((via[(nb(-1, 0), rank)], T.acc[:, 0:2, p0:p1, :], W, T.ht[:, :, p0 + dq:p1 + dq, :]))
            if a == 2:
                rows.append((via[(nb(1, 0), rank)], T.acc[:, 6:8, p0:p1, :], W, T.hb[:, :, p0 + dq:p1 + dq, :]))
            if b != 1:
                src = [nb(0, dq)] + ([nb(a - 1, dq)] if a != 1 else [])
                kind = KINDS[max(KINDS.index(via[(s, rank)]) for s in src)]
                if b == 0:
                    strips.append((kind, T.acce[:, 0:8, 0:1, :], W, T.hl[:, 6 + 2 * a:14 + 2 * a, 1:2, :]))
                else:
                    strips.append((kind, T.acce[:, 0:8, 1:2, :], W, T.hr[:, 6 + 2 * a:14 + 2 * a, 0:1, :]))
        own.append(part)
    nmain = sum(len(p) for p in own) + len(rows)
    te = g.tensor
    te.wait_ge(S.ldx, 16)
    k = 0
    for i, part in enumerate(own):
        te.wait_ge(S["lw%d" % i], 16)
        for (out, W, rhs) in part:
            te.matmul(out, W, rhs, start=(k == 0), stop=False).then_inc(S.mm, 1)
            k += 1
    for kind in ("dtb", "ftb"):
        if (core, kind) in arrive:
            te.wait_ge(S[kind], arrive[(core, kind)])
            for (kd, out, W, rhs) in rows:
                if kd == kind:
                    k += 1
                    te.matmul(out, W, rhs, start=False, stop=(k == nmain)).then_inc(S.mm, 1)
    te.wait_ge(S.zed, 1)
    k = 0
    for kind in ("dpk", "fpk"):
        if (core, kind) in arrive:
            te.wait_ge(S[kind], arrive[(core, kind)])
            for (kd, out, W, rhs) in strips:
                if kd == kind:
                    k += 1
                    te.matmul(out, W, rhs, start=(k == 1), stop=(k == len(strips))).then_inc(S.me, 1)

    g.vector.wait_ge(S.mm, nmain)
    g.vector.tensor_copy(T.te[:, :, :, :], T.acc[:, 0:8, 0:16:15, :]).then_inc(S.cpe, 1)
    g.vector.tensor_copy(T.ys[:, :, 1:15, :], T.acc[:, 0:8, 1:15, :]).then_inc(S.cpd, 1)
    g.vector.wait_ge(S.me, len(strips))
    g.vector.wait_ge(S.cpe, 1)
    g.vector.tensor_tensor(T.ys[:, :, 0:16:15, :], T.acce[:, 0:8, :, :], T.te[:, :, :, :],
                           AluOpType.add).then_inc(S.cpd, 1)
    g.sync.wait_ge(S.cpd, 2)
    g.sync.dma_start(T.y[:, :], T.ys[:, :, :, :]).then_inc(S.std, 16)
    g.sync.wait_ge(S.std, 16)
    g.wait_ge(S.sent, nsent)
